import numpy as np
import ml_dtypes


def mxq(x, axis, fmt="e4m3"):
    dtype, down = {"e4m3": (ml_dtypes.float8_e4m3fn, 7), "e5m2": (ml_dtypes.float8_e5m2, 14)}[fmt]
    v = np.moveaxis(np.asarray(x, np.float32).astype(ml_dtypes.bfloat16).astype(np.float64), axis, -1)
    blocks = v.reshape(v.shape[:-1] + (-1, 32))
    amax = np.abs(blocks).max(-1, keepdims=True)
    byte = np.maximum(np.where(amax > 0, np.frexp(amax)[1] - 1 + 127, 0) - down, 1)
    scale = np.exp2(byte - 127.0)
    codes = (blocks / scale).astype(np.float32).astype(dtype).astype(np.float64)
    return np.moveaxis((codes * scale).reshape(v.shape), -1, axis)


WIDE = False


def mx_kscale(k):
    if not WIDE:
        return np.ones(k)
    levels = np.array([10, -10, 5, -5, 0])
    if k % 512:
        return np.exp2(np.random.permutation(np.resize(levels, k // 32))).repeat(32)
    a = np.empty((k // 512, 16))
    for p in range(k // 512):
        a[p, :8] = np.random.permutation(np.resize(levels, 8))
        for g in range(8):
            far = levels[np.abs(levels - a[p, g]) >= 10]
            a[p, g + 8] = far[np.random.randint(len(far))]
    return np.exp2(a.ravel()).repeat(32)


def f64(x):
    return np.asarray(x).astype(np.float64)


def striped(idx):
    return np.tile(idx.reshape(-1, 16).T, (8, 1)).astype(np.uint16)


def unstriped(offs):
    return offs[:16].T.reshape(-1).astype(np.int64)


def striped8(idx):
    return np.concatenate([x.reshape(-1, 16).T for x in idx]).astype(np.uint16)


def runs(offs, k):
    lists = np.stack([offs[16 * r : 16 * r + 16].T.reshape(-1) for r in range(8)]).astype(np.int64)
    return lists[np.arange(k) % 512 // 64]


def pack_weight(w):
    k, n = w.shape
    w = f64(np.asarray(w, np.float32).astype(ml_dtypes.bfloat16)).reshape(k // 32, 32, n)
    amax = np.abs(w).max(1)
    byte = np.clip(np.where(amax > 0, np.frexp(amax)[1] - 1 + 127 - 7, 1), 1, 254)
    scaled = (w * np.exp2(127.0 - byte)[:, None, :]).reshape(k, n).astype(np.float32)
    words = np.ascontiguousarray(scaled.reshape(k // 512, 128, 4, n).transpose(0, 1, 3, 2)).astype(ml_dtypes.float8_e4m3fn).view(np.uint8)
    return words, np.ascontiguousarray(byte.astype(np.uint8).reshape(k // 512, 16, n))


def unpack_weight(words, scales):
    g, p, n, _ = words.shape
    vals = np.ascontiguousarray(words).view(ml_dtypes.float8_e4m3fn).astype(np.float64) * np.repeat(np.exp2(scales.astype(np.float64) - 127.0), 8, axis=1)[..., None]
    return vals.transpose(0, 1, 3, 2).reshape(g * 512, n)


E2M1 = np.array([0.0, 0.5, 1.0, 1.5, 2.0, 3.0, 4.0, 6.0, -0.0, -0.5, -1.0, -1.5, -2.0, -3.0, -4.0, -6.0])


def pack_fp4(w):
    k, n = w.shape
    w = f64(np.asarray(w, np.float32).astype(ml_dtypes.bfloat16)).reshape(k // 32, 32, n)
    amax = np.abs(w).max(1)
    mant, ex = np.frexp(amax / 6.0)
    byte = np.clip(np.where(amax > 0, np.where(mant > 0.5, ex, ex - 1) + 127, 1), 1, 254)
    scaled = (w * np.exp2(127.0 - byte)[:, None, :]).reshape(k, n).astype(np.float32)
    c = np.ascontiguousarray(scaled.reshape(k // 512, 128, 4, n).transpose(0, 1, 3, 2)).astype(ml_dtypes.float4_e2m1fn).view(np.uint8) & 0xF
    words = (c[..., 0::2] | (c[..., 1::2] << 4)).reshape(k // 512, 128, 2 * n)
    return np.ascontiguousarray(words), np.ascontiguousarray(byte.astype(np.uint8).reshape(k // 512, 16, n))


def unpack_fp4(words, scales):
    g, _, n = scales.shape
    words = np.ascontiguousarray(words).reshape(g, 128, n, 2)
    nib = np.empty((g, 128, n, 4), np.uint8)
    nib[..., 0::2] = words & 0xF
    nib[..., 1::2] = words >> 4
    vals = E2M1[nib] * np.repeat(np.exp2(scales.astype(np.float64) - 127.0), 8, axis=1)[..., None]
    return vals.transpose(0, 1, 3, 2).reshape(g * 512, n)


def sigmoid(v):
    return 1.0 / (1.0 + np.exp(-np.maximum(v, -700.0)))

def planes(y):
    n, m = y.shape
    v = y.astype(np.float32).astype(ml_dtypes.bfloat16).astype(np.float64).reshape(n // 32, 32, m)
    top = np.abs(v).max(1)
    byte = np.clip(np.where(top > 0, np.frexp(top)[1] - 1 + 127 - 7, 1), 1, 254)
    codes = (v * np.exp2(127.0 - byte)[:, None, :]).reshape(n, m).astype(np.float32).astype(ml_dtypes.float8_e4m3fn).view(np.uint8)
    words = codes.reshape(n // 512, 128, 4, m).transpose(0, 1, 3, 2)
    return np.ascontiguousarray(words), np.ascontiguousarray(byte.astype(np.uint8).reshape(n // 512, 16, m))


K, T, S, N, H, W = 512, 2048, 512, 512, 512, 1024


def setup_inputs():
    n = np.random.standard_normal
    s = mx_kscale(K)[:, None]
    u = mx_kscale(H)
    packed_xT = pack_weight(n((K, T)) * s)
    packed_w1 = pack_fp4(n((K, H)) / np.sqrt(K) / s)
    packed_w2 = pack_fp4(n((H, N)) / np.sqrt(2 * H) / u[:, None])
    packed_w3 = pack_fp4(n((K, N)) / np.sqrt(2 * K) / s)
    return {
        "x_words": packed_xT[0],
        "x_scales": packed_xT[1],
        "w1_words": packed_w1[0],
        "w1_scales": packed_w1[1],
        "gn": (np.random.uniform(0.5, 1.5, (H, 1)) * u[:, None]).astype(np.float32),
        "w2_words": packed_w2[0],
        "w2_scales": packed_w2[1],
        "w3_words": packed_w3[0],
        "w3_scales": packed_w3[1],
        "offs": striped8(np.random.randint(0, T, (8, S))),
        "n1": striped(np.random.randint(0, S, W)),
        "two": striped(np.random.permutation(T)[:S]),
        "n2": striped8(np.stack([np.random.permutation(S) for _ in range(8)])),
        "n3": striped8(np.stack([np.random.permutation(S) for _ in range(8)])),
    }


def reference(x_words, x_scales, w1_words, w1_scales, gn, w2_words, w2_scales, w3_words, w3_scales, offs, n1, two, n2, n3):
    xq = unpack_weight(x_words, x_scales)[np.arange(K)[:, None], runs(offs, K)]
    y = unpack_fp4(w1_words, w1_scales).T @ xq
    mb = y[:, unstriped(n1)]
    mn = mb.reshape(H, S, 2).min(axis=2)
    mx = mb.reshape(H, S, 2).max(axis=2)
    z = f64(gn) * ((y - mn) * sigmoid(mx))
    x_two = unpack_weight(x_words, x_scales)[:, unstriped(two)]
    h = unpack_fp4(w2_words, w2_scales).T @ mxq(z, 0, "e4m3") + unpack_fp4(w3_words, w3_scales).T @ x_two
    st = h - (h[np.arange(N)[:, None], runs(n2, N)])
    out_0 = np.maximum(st, st[np.arange(N)[:, None], runs(n3, N)])
    return (out_0,) + planes(out_0)

@@ -1,0 +1,242 @@
+from contextlib import ExitStack
+
+import concourse.mybir as mybir
+
+F32 = mybir.dt.float32
+BF16 = mybir.dt.bfloat16
+I32 = mybir.dt.int32
+U32 = mybir.dt.uint32
+U16 = mybir.dt.uint16
+U8 = mybir.dt.uint8
+FP8X4 = mybir.dt.float8_e4m3fn_x4
+FP4X4 = mybir.dt.float4_e2m1fn_x4
+ALU = mybir.AluOpType
+ACT = mybir.ActivationFunctionType
+
+P = 128
+PACK = 4
+T = 2048
+S = 512
+FLOPS = 3 * 2 * 512 * 512 * 512
+
+Z_CHUNKS = (256, 128, 128)
+OUT_CHUNKS = (256, 128, 128)
+HALF = 256
+PAD = 16
+RING = 3
+Y_ON_SCALAR = (0, 2)
+
+
+def spans(widths):
+    out = []
+    start = 0
+    for w in widths:
+        out.append((start, w))
+        start = start + w
+    return out
+
+
+def tile_picked_hmixghardhopmx_none_po_kernel(
+    tc, x_words, x_scales, w1_words, w1_scales, gn, w2_words, w2_scales, w3_words, w3_scales,
+    offs, n1, two, n2, n3, out_0, out_1, out_2,
+):
+    nc = tc.nc
+    with ExitStack() as ctx:
+        keep = ctx.enter_context(tc.tile_pool(name="keep", bufs=1))
+        ring = ctx.enter_context(tc.tile_pool(name="ring", bufs=RING))
+        psum = ctx.enter_context(tc.psum_pool(name="psum", bufs=1))
+
+        def sb(shape, dtype, name):
+            return keep.tile(shape, dtype, name=name, align_bytes=64)
+
+        offs_t = sb([P, 32], U16, "offs_t")
+        n1_t = sb([P, 64], U16, "n1_t")
+        two_t = sb([P, 32], U16, "two_t")
+        n2_t = sb([P, 32], U16, "n2_t")
+        n3_t = sb([P, 32], U16, "n3_t")
+        xw = sb([P, T], U32, "xw")
+        xs = sb([P, T], U8, "xs")
+        gain = sb([P, PACK], F32, "gain")
+
+        def load_weight(words, scales, word_queue, scale_queue):
+            raw_w = sb([P, 2 * S], U8, "raw_w")
+            raw_s = sb([P, S], U8, "raw_s")
+            word_queue.dma_start(out=raw_w[:].bitcast(I32), in_=words[0].bitcast(I32))
+            for q in range(4):
+                rows = scales[0][4 * q : 4 * q + 4, :].bitcast(I32)
+                scale_queue.dma_start(
+                    out=raw_s[32 * q : 32 * q + 32, :].bitcast(I32), in_=rows.unsqueeze(0).to_broadcast([8, 4, S // 4])
+                )
+            return raw_w, raw_s
+
+        def deal(raw, name):
+            raw_w, raw_s = raw
+            words = sb([P, 2 * S], U8, name + "_w")
+            scales = sb([P, S], U8, name + "_s")
+            nc.vector.tensor_copy(
+                out=words[:].rearrange("p (t m b) -> p t m b", t=PACK, b=2),
+                in_=raw_w[:].rearrange("p (m t b) -> p t m b", t=PACK, b=2),
+            )
+            nc.vector.tensor_copy(
+                out=scales[:].rearrange("p (t m) -> p t m", t=PACK),
+                in_=raw_s[:].rearrange("p (m t) -> p t m", t=PACK),
+            )
+            return words, scales
+
+        def stationary(weight, t):
+            words, scales = weight
+            return dict(
+                lhsT=words[:, 2 * P * t : 2 * P * (t + 1)].bitcast(FP4X4),
+                lhsT_scale=scales[:, P * t : P * (t + 1)],
+            )
+
+        def pick_scales(lists, name, queue):
+            got = sb([P, S], U8, name + "_got")
+            placed = sb([P, S], U8, name + "_placed")
+            nc.vector.tensor_copy(out=got[:], in_=xs[:].indirect(lists[:]))
+            nc.vector.tensor_copy(out=placed[:].bitcast(I32), in_=got[:].bitcast(I32))
+            for b in range(2):
+                queue.dma_start(out=placed[2 + b : P : 32, :].bitcast(I32), in_=got[16 + b : P : 32, :].bitcast(I32))
+            return placed
+
+        def pick_words(lists, name):
+            got = sb([P, S], U32, name)
+            nc.vector.tensor_copy(out=got[:], in_=xw[:].indirect(lists[:]))
+            return got
+
+        y = [sb([P, S + PAD], F32, "y%d" % t) for t in range(PACK)]
+
+        nc.sync.dma_start(out=offs_t[:], in_=offs)
+        for b in range(2):
+            rows = x_scales[0][b:16:2, :].bitcast(I32)
+            nc.scalar.dma_start(out=xs[b:P:2, :].bitcast(I32), in_=rows.unsqueeze(1).to_broadcast([8, 8, T // 4]))
+        nc.sync.dma_start(out=xw[:].bitcast(I32), in_=x_words[0].rearrange("p n r -> p (n r)").bitcast(I32))
+        raw1 = load_weight(w1_words, w1_scales, nc.gpsimd, nc.scalar)
+        nc.sync.dma_start(out=two_t[:], in_=two)
+        nc.sync.dma_start(out=n1_t[:], in_=n1)
+        nc.sync.dma_start(out=n2_t[:], in_=n2)
+        nc.sync.dma_start(out=n3_t[:], in_=n3)
+        nc.gpsimd.dma_start(out=gain[:], in_=gn.rearrange("(p t) o -> p (t o)", t=PACK))
+        for t in range(PACK):
+            nc.gpsimd.memset(y[t][:, S:], 0.0)
+
+        xq_s = pick_scales(offs_t, "xq_s", nc.scalar)
+        w1 = deal(raw1, "w1")
+        xq_w = pick_words(offs_t, "xq_w")
+        raw3 = load_weight(w3_words, w3_scales, nc.sync, nc.sync)
+
+        y_ps = [psum.tile([P, S], F32, name="y_ps%d" % t) for t in range(PACK)]
+        h_ps = [psum.tile([P, S], F32, name="h_ps%d" % t) for t in range(PACK)]
+        for t in range(PACK):
+            nc.tensor.matmul_mx(out=y_ps[t][:], rhs=xq_w[:].bitcast(FP8X4), rhs_scale=xq_s[:], start=True, stop=True, **stationary(w1, t))
+        x2_w = pick_words(two_t, "x2_w")
+        for t in range(PACK):
+            if t not in Y_ON_SCALAR:
+                nc.vector.tensor_copy(out=y[t][:, :S], in_=y_ps[t][:])
+        x2_s = pick_scales(two_t, "x2_s", nc.sync)
+        w3 = deal(raw3, "w3")
+        raw2 = load_weight(w2_words, w2_scales, nc.sync, nc.sync)
+        for t in range(PACK):
+            nc.tensor.matmul_mx(out=h_ps[t][:], rhs=x2_w[:].bitcast(FP8X4), rhs_scale=x2_s[:], start=True, stop=False, **stationary(w3, t))
+        w2 = deal(raw2, "w2")
+
+        z_codes = sb([P, S], U32, "z_codes")
+        z_scales = sb([P, S], U8, "z_scales")
+        chunks = spans(Z_CHUNKS)
+        zt = [sb([P, PACK, w], BF16, "zt%d" % c) for c, (j0, w) in enumerate(chunks)]
+        zi = [sb([P, w, PACK], BF16, "zi%d" % c) for c, (j0, w) in enumerate(chunks)]
+        mn = {}
+        sg = {}
+        df = {}
+
+        def fetch(c, t):
+            j0, w = chunks[c]
+            if c == 0 and t in Y_ON_SCALAR:
+                nc.scalar.copy(out=y[t][:, :S], in_=y_ps[t][:])
+            unit = ring.tile([P, 3 * w], F32, name="unit", align_bytes=64)
+            pairs = unit[:, : 2 * w]
+            mx = unit[:, 2 * w :]
+            mn[c, t] = sb([P, w], F32, "mn%d_%d" % (c, t))
+            sg[c, t] = sb([P, w], F32, "sg%d_%d" % (c, t))
+            nc.scalar.activation(pairs, y[t][:].indirect(n1_t[:, j0 // 8 : (j0 + w) // 8]), ACT.Copy)
+            nc.vector.tensor_tensor(mx, pairs[:, 0::2], pairs[:, 1::2], ALU.max)
+            nc.vector.tensor_tensor(mn[c, t][:], pairs[:, 0::2], pairs[:, 1::2], ALU.min)
+            nc.scalar.activation(sg[c, t][:], mx, ACT.Sigmoid)
+
+        def subtract(c, t):
+            j0, w = chunks[c]
+            df[c, t] = sb([P, w], F32, "df%d_%d" % (c, t))
+            nc.vector.tensor_tensor(df[c, t][:], y[t][:, j0 : j0 + w], mn[c, t][:], ALU.subtract)
+
+        def gate(c, t):
+            nc.vector.scalar_tensor_tensor(zt[c][:, t], df[c, t][:], gain[:, t : t + 1], sg[c, t][:], ALU.mult, ALU.mult)
+
+        def interleave(c):
+            nc.vector.tensor_copy(
+                out=zi[c][:].rearrange("p (c i) t -> p c t i", i=4), in_=zt[c][:].rearrange("p t (c i) -> p c t i", i=4)
+            )
+
+        def multiply(c):
+            j0, w = chunks[c]
+            cols = slice(j0, j0 + w)
+            nc.vector.quantize_mx(
+                out=z_codes[:, cols].bitcast(FP8X4), scales=z_scales[:, cols], in_=zi[c][:].rearrange("p j t -> p (j t)")
+            )
+            for t in range(PACK):
+                nc.tensor.matmul_mx(
+                    out=h_ps[t][:, cols], rhs=z_codes[:, cols].bitcast(FP8X4), rhs_scale=z_scales[:, cols],
+                    start=False, stop=(c == len(chunks) - 1), **stationary(w2, t)
+                )
+
+        units = [(c, t) for c in range(len(chunks)) for t in range(PACK)]
+        for u, (c, t) in enumerate(units):
+            fetch(c, t)
+            if u > 0:
+                gate(*units[u - 1])
+            subtract(c, t)
+            if c > 0 and t == 0:
+                interleave(c - 1)
+            if c > 0 and t == 1:
+                multiply(c - 1)
+        gate(*units[-1])
+        interleave(len(chunks) - 1)
+        multiply(len(chunks) - 1)
+
+        h = [sb([P, S], F32, "h%d" % t) for t in range(PACK)]
+        hop = [sb([P, S], F32, "hop%d" % t) for t in range(PACK)]
+        st = [sb([P, S], F32, "st%d" % t) for t in range(PACK)]
+        for t in range(PACK):
+            if t == 0:
+                nc.scalar.copy(out=h[t][:], in_=h_ps[t][:])
+            else:
+                nc.vector.tensor_copy(out=h[t][:], in_=h_ps[t][:])
+        for t in range(PACK):
+            for j0 in range(0, S, HALF):
+                nc.scalar.activation(
+                    hop[t][:, j0 : j0 + HALF], h[t][:].indirect(n2_t[:, j0 // 16 : (j0 + HALF) // 16]), ACT.Copy
+                )
+            nc.vector.tensor_tensor(st[t][:], h[t][:], hop[t][:], ALU.subtract)
+
+        o_codes = sb([P, S], U32, "o_codes")
+        o_scales = sb([P, S], U8, "o_scales")
+        out_rows = out_0.rearrange("(p t) j -> p t j", t=PACK)
+        out_words = out_1[0].rearrange("p n r -> p (n r)").bitcast(I32)
+        for c, (j0, w) in enumerate(spans(OUT_CHUNKS)):
+            cols = slice(j0, j0 + w)
+            far = sb([P, PACK, w], F32, "far%d" % c)
+            res = sb([P, PACK, w], F32, "res%d" % c)
+            ri = sb([P, w, PACK], BF16, "ri%d" % c)
+            for t in range(PACK):
+                nc.scalar.activation(far[:, t], st[t][:].indirect(n3_t[:, j0 // 16 : (j0 + w) // 16]), ACT.Copy)
+                nc.vector.tensor_tensor(res[:, t], st[t][:, cols], far[:, t], ALU.max)
+            nc.sync.dma_start(out=out_rows[:, :, cols], in_=res[:])
+            nc.vector.tensor_copy(
+                out=ri[:].rearrange("p (c i) t -> p c t i", i=4), in_=res[:].rearrange("p t (c i) -> p c t i", i=4)
+            )
+            nc.vector.quantize_mx(
+                out=o_codes[:, cols].bitcast(FP8X4), scales=o_scales[:, cols], in_=ri[:].rearrange("p j t -> p (j t)")
+            )
+            nc.sync.dma_start(out=out_words[:, cols], in_=o_codes[:, cols].bitcast(I32))
+        for q in range(4):
+            queue = nc.scalar if q % 2 else nc.sync
+            queue.dma_start(out=out_2[0][4 * q : 4 * q + 4, :].bitcast(I32), in_=o_scales[32 * q : 32 * q + 4, :].bitcast(I32))

@@ -19,12 +19,13 @@ T = 2048
 S = 512
 FLOPS = 3 * 2 * 512 * 512 * 512
 
-Z_CHUNKS = (256, 128, 128)
+UNITS = ((0, 0, 256), (1, 0, 256), (2, 0, 256), (3, 0, 256), (0, 256, 256), (1, 256, 256), (2, 256, 256), (3, 256, 128), (3, 384, 128))
+GATHER = 256
 OUT_CHUNKS = (256, 128, 128)
 HALF = 256
 PAD = 16
-RING = 3
-Y_ON_SCALAR = (0, 2)
+RING = 2
+Y_ON_SCALAR = (0,)
 
 
 def spans(widths):
@@ -58,30 +59,28 @@ def tile_picked_hmixghardhopmx_none_po_kernel(
         xs = sb([P, T], U8, "xs")
         gain = sb([P, PACK], F32, "gain")
 
-        def load_weight(words, scales, word_queue, scale_queue):
-            raw_w = sb([P, 2 * S], U8, "raw_w")
-            raw_s = sb([P, S], U8, "raw_s")
-            word_queue.dma_start(out=raw_w[:].bitcast(I32), in_=words[0].bitcast(I32))
+        def load_words(queue, words, raw):
+            queue.dma_start(out=raw.bitcast(I32), in_=words[0].bitcast(I32))
+
+        def load_scales(queue, scales, raw):
             for q in range(4):
                 rows = scales[0][4 * q : 4 * q + 4, :].bitcast(I32)
-                scale_queue.dma_start(
-                    out=raw_s[32 * q : 32 * q + 32, :].bitcast(I32), in_=rows.unsqueeze(0).to_broadcast([8, 4, S // 4])
-                )
-            return raw_w, raw_s
+                queue.dma_start(out=raw[32 * q : 32 * q + 32, :].bitcast(I32), in_=rows.unsqueeze(0).to_broadcast([8, 4, S // 4]))
 
-        def deal(raw, name):
-            raw_w, raw_s = raw
-            words = sb([P, 2 * S], U8, name + "_w")
-            scales = sb([P, S], U8, name + "_s")
-            nc.vector.tensor_copy(
-                out=words[:].rearrange("p (t m b) -> p t m b", t=PACK, b=2),
-                in_=raw_w[:].rearrange("p (m t b) -> p t m b", t=PACK, b=2),
+        def deal_words(engine, raw, name):
+            words = sb([P, 2 * S], U8, name)
+            engine.tensor_copy(
+                out=words[:].rearrange("p (t m b) -> p t b m", t=PACK, b=2),
+                in_=raw.rearrange("p (m t b) -> p t b m", t=PACK, b=2),
             )
-            nc.vector.tensor_copy(
-                out=scales[:].rearrange("p (t m) -> p t m", t=PACK),
-                in_=raw_s[:].rearrange("p (m t) -> p t m", t=PACK),
+            return words
+
+        def deal_scales(engine, raw, name):
+            scales = sb([P, S], U8, name)
+            engine.tensor_copy(
+                out=scales[:].rearrange("p (t m) -> p t m", t=PACK), in_=raw.rearrange("p (m t) -> p t m", t=PACK)
             )
-            return words, scales
+            return scales
 
         def stationary(weight, t):
             words, scales = weight
@@ -90,13 +89,13 @@ def tile_picked_hmixghardhopmx_none_po_kernel(
                 lhsT_scale=scales[:, P * t : P * (t + 1)],
             )
 
-        def pick_scales(lists, name, queue):
-            got = sb([P, S], U8, name + "_got")
+        def pick_scales(lists, name, queue, stage):
+            got = sb([P, S], U8, stage)
             placed = sb([P, S], U8, name + "_placed")
             nc.vector.tensor_copy(out=got[:], in_=xs[:].indirect(lists[:]))
             nc.vector.tensor_copy(out=placed[:].bitcast(I32), in_=got[:].bitcast(I32))
             for b in range(2):
-                queue.dma_start(out=placed[2 + b : P : 32, :].bitcast(I32), in_=got[16 + b : P : 32, :].bitcast(I32))
+                queue[b].dma_start(out=placed[2 + b : P : 32, :].bitcast(I32), in_=got[16 + b : P : 32, :].bitcast(I32))
             return placed
 
         def pick_words(lists, name):
@@ -105,102 +104,137 @@ def tile_picked_hmixghardhopmx_none_po_kernel(
             return got
 
         y = [sb([P, S + PAD], F32, "y%d" % t) for t in range(PACK)]
+        warm = sb([P, 2], F32, "warm")
+        nc.vector.memset(warm[:, 0:1], 0.0)
+
+        def load_token_scales(queue, b):
+            rows = x_scales[0][b:16:2, :].bitcast(I32)
+            queue.dma_start(out=xs[b:P:2, :].bitcast(I32), in_=rows.unsqueeze(1).to_broadcast([8, 8, T // 4]))
 
         nc.sync.dma_start(out=offs_t[:], in_=offs)
-        for b in range(2):
-            rows = x_scales[0][b:16:2, :].bitcast(I32)
-            nc.scalar.dma_start(out=xs[b:P:2, :].bitcast(I32), in_=rows.unsqueeze(1).to_broadcast([8, 8, T // 4]))
-        nc.sync.dma_start(out=xw[:].bitcast(I32), in_=x_words[0].rearrange("p n r -> p (n r)").bitcast(I32))
-        raw1 = load_weight(w1_words, w1_scales, nc.gpsimd, nc.scalar)
+        load_token_scales(nc.scalar, 1)
+        load_token_scales(nc.sync, 0)
+        raw_w1 = sb([P, 2 * S], U8, "raw_w")
+        load_words(nc.scalar, w1_words, raw_w1[:])
         nc.sync.dma_start(out=two_t[:], in_=two)
         nc.sync.dma_start(out=n1_t[:], in_=n1)
         nc.sync.dma_start(out=n2_t[:], in_=n2)
-        nc.sync.dma_start(out=n3_t[:], in_=n3)
+        nc.sync.dma_start(out=xw[:].bitcast(I32), in_=x_words[0].rearrange("p n r -> p (n r)").bitcast(I32))
+        raw_s1 = sb([P, S], U8, "raw_s1")
+        load_scales(nc.sync, w1_scales, raw_s1[:])
         nc.gpsimd.dma_start(out=gain[:], in_=gn.rearrange("(p t) o -> p (t o)", t=PACK))
+        nc.scalar.activation(warm[:, 1:2], warm[:, 0:1], ACT.Sigmoid)
         for t in range(PACK):
-            nc.gpsimd.memset(y[t][:, S:], 0.0)
+            nc.vector.memset(y[t][:, S:], 0.0)
 
-        xq_s = pick_scales(offs_t, "xq_s", nc.scalar)
-        w1 = deal(raw1, "w1")
-        xq_w = pick_words(offs_t, "xq_w")
-        raw3 = load_weight(w3_words, w3_scales, nc.sync, nc.sync)
+        xq_s = pick_scales(offs_t, "xq_s", (nc.scalar, nc.scalar), "xq_s_got")
+        nc.sync.dma_start(out=n3_t[:], in_=n3)
+        w1_w = deal_words(nc.gpsimd, raw_w1[:], "w1_w")
+        x2_s = pick_scales(two_t, "x2_s", (nc.sync, nc.sync), "x2_s_got")
+        xq_w = sb([P, S], U32, "xq_w")
+        for j0 in range(0, S, HALF):
+            nc.vector.tensor_copy(out=xq_w[:, j0 : j0 + HALF], in_=xw[:].indirect(offs_t[:, j0 // 16 : (j0 + HALF) // 16]))
+        w1 = (w1_w, deal_scales(nc.gpsimd, raw_s1[:], "w1_s"))
+        raw_32 = sb([P, 6 * S], U8, "raw_w")
+        raw_w32 = raw_32[:, : 4 * S]
+        raw_s32 = raw_32[:, 4 * S :]
+        load_words(nc.sync, w3_words, raw_w32[:, : 2 * S])
+        load_words(nc.sync, w2_words, raw_w32[:, 2 * S :])
+        load_scales(nc.sync, w3_scales, raw_s32[:, :S])
+        load_scales(nc.sync, w2_scales, raw_s32[:, S:])
+        w3_w = deal_words(nc.gpsimd, raw_w32[:, : 2 * S], "w3_w")
+        w2_w = deal_words(nc.gpsimd, raw_w32[:, 2 * S :], "w2_w")
 
         y_ps = [psum.tile([P, S], F32, name="y_ps%d" % t) for t in range(PACK)]
-        h_ps = [psum.tile([P, S], F32, name="h_ps%d" % t) for t in range(PACK)]
-        for t in range(PACK):
+        first = psum.tile([P, HALF], F32, name="h_ps3")
+        nc.tensor.matmul_mx(
+            out=first[:], rhs=xq_w[:, :HALF].bitcast(FP8X4), rhs_scale=xq_s[:, :HALF], start=True, stop=True, **stationary(w1, 0)
+        )
+        nc.scalar.copy(out=y[0][:, :HALF], in_=first[:])
+        nc.tensor.matmul_mx(
+            out=y_ps[0][:, HALF:], rhs=xq_w[:, HALF:].bitcast(FP8X4), rhs_scale=xq_s[:, HALF:], start=True, stop=True, **stationary(w1, 0)
+        )
+        nc.scalar.copy(out=y[0][:, HALF:S], in_=y_ps[0][:, HALF:])
+        for t in range(1, PACK):
             nc.tensor.matmul_mx(out=y_ps[t][:], rhs=xq_w[:].bitcast(FP8X4), rhs_scale=xq_s[:], start=True, stop=True, **stationary(w1, t))
+        h_ps = [psum.tile([P, S], F32, name="h_ps%d" % t) for t in range(PACK)]
         x2_w = pick_words(two_t, "x2_w")
         for t in range(PACK):
             if t not in Y_ON_SCALAR:
                 nc.vector.tensor_copy(out=y[t][:, :S], in_=y_ps[t][:])
-        x2_s = pick_scales(two_t, "x2_s", nc.sync)
-        w3 = deal(raw3, "w3")
-        raw2 = load_weight(w2_words, w2_scales, nc.sync, nc.sync)
+        w3 = (w3_w, deal_scales(nc.vector, raw_s32[:, :S], "w3_s"))
         for t in range(PACK):
             nc.tensor.matmul_mx(out=h_ps[t][:], rhs=x2_w[:].bitcast(FP8X4), rhs_scale=x2_s[:], start=True, stop=False, **stationary(w3, t))
-        w2 = deal(raw2, "w2")
+        w2 = (w2_w, deal_scales(nc.vector, raw_s32[:, S:], "w2_s"))
 
         z_codes = sb([P, S], U32, "z_codes")
         z_scales = sb([P, S], U8, "z_scales")
-        chunks = spans(Z_CHUNKS)
-        zt = [sb([P, PACK, w], BF16, "zt%d" % c) for c, (j0, w) in enumerate(chunks)]
-        zi = [sb([P, w, PACK], BF16, "zi%d" % c) for c, (j0, w) in enumerate(chunks)]
+        zt = sb([P, PACK, S], BF16, "zt")
         mn = {}
         sg = {}
         df = {}
+        zi = {}
 
-        def fetch(c, t):
-            j0, w = chunks[c]
-            if c == 0 and t in Y_ON_SCALAR:
+        def fetch(u):
+            t, j0, w = UNITS[u]
+            if j0 == 0 and t > 0 and t in Y_ON_SCALAR:
                 nc.scalar.copy(out=y[t][:, :S], in_=y_ps[t][:])
             unit = ring.tile([P, 3 * w], F32, name="unit", align_bytes=64)
             pairs = unit[:, : 2 * w]
             mx = unit[:, 2 * w :]
-            mn[c, t] = sb([P, w], F32, "mn%d_%d" % (c, t))
-            sg[c, t] = sb([P, w], F32, "sg%d_%d" % (c, t))
-            nc.scalar.activation(pairs, y[t][:].indirect(n1_t[:, j0 // 8 : (j0 + w) // 8]), ACT.Copy)
+            mn[u] = sb([P, w], F32, "mn%d" % u)
+            sg[u] = sb([P, w], F32, "sg%d" % u)
+            step = min(w, GATHER)
+            for a in range(0, w, step):
+                nc.scalar.activation(
+                    pairs[:, 2 * a : 2 * (a + step)], y[t][:].indirect(n1_t[:, (j0 + a) // 8 : (j0 + a + step) // 8]), ACT.Copy
+                )
             nc.vector.tensor_tensor(mx, pairs[:, 0::2], pairs[:, 1::2], ALU.max)
-            nc.vector.tensor_tensor(mn[c, t][:], pairs[:, 0::2], pairs[:, 1::2], ALU.min)
-            nc.scalar.activation(sg[c, t][:], mx, ACT.Sigmoid)
+            nc.vector.tensor_tensor(mn[u][:], pairs[:, 0::2], pairs[:, 1::2], ALU.min)
+            nc.scalar.activation(sg[u][:], mx, ACT.Sigmoid)
 
-        def subtract(c, t):
-            j0, w = chunks[c]
-            df[c, t] = sb([P, w], F32, "df%d_%d" % (c, t))
-            nc.vector.tensor_tensor(df[c, t][:], y[t][:, j0 : j0 + w], mn[c, t][:], ALU.subtract)
+        def subtract(u):
+            t, j0, w = UNITS[u]
+            df[u] = sb([P, w], F32, "df%d" % u)
+            nc.vector.tensor_tensor(df[u][:], y[t][:, j0 : j0 + w], mn[u][:], ALU.subtract)
 
-        def gate(c, t):
-            nc.vector.scalar_tensor_tensor(zt[c][:, t], df[c, t][:], gain[:, t : t + 1], sg[c, t][:], ALU.mult, ALU.mult)
+        def gate(u):
+            t, j0, w = UNITS[u]
+            nc.vector.scalar_tensor_tensor(zt[:, t, j0 : j0 + w], df[u][:], gain[:, t : t + 1], sg[u][:], ALU.mult, ALU.mult)
 
-        def interleave(c):
+        def interleave(u):
+            t, j0, w = UNITS[u]
+            zi[u] = sb([P, w, PACK], BF16, "zi%d" % u)
             nc.vector.tensor_copy(
-                out=zi[c][:].rearrange("p (c i) t -> p c t i", i=4), in_=zt[c][:].rearrange("p t (c i) -> p c t i", i=4)
+                out=zi[u][:].rearrange("p (c i) t -> p c t i", i=4),
+                in_=zt[:, :, j0 : j0 + w].rearrange("p t (c i) -> p c t i", i=4),
             )
 
-        def multiply(c):
-            j0, w = chunks[c]
+        def multiply(u):
+            t, j0, w = UNITS[u]
             cols = slice(j0, j0 + w)
             nc.vector.quantize_mx(
-                out=z_codes[:, cols].bitcast(FP8X4), scales=z_scales[:, cols], in_=zi[c][:].rearrange("p j t -> p (j t)")
+                out=z_codes[:, cols].bitcast(FP8X4), scales=z_scales[:, cols], in_=zi[u][:].rearrange("p j t -> p (j t)")
             )
-            for t in range(PACK):
+            for m in range(PACK):
                 nc.tensor.matmul_mx(
-                    out=h_ps[t][:, cols], rhs=z_codes[:, cols].bitcast(FP8X4), rhs_scale=z_scales[:, cols],
-                    start=False, stop=(c == len(chunks) - 1), **stationary(w2, t)
+                    out=h_ps[m][:, cols], rhs=z_codes[:, cols].bitcast(FP8X4), rhs_scale=z_scales[:, cols],
+                    start=False, stop=(u == len(UNITS) - 1), **stationary(w2, m)
                 )
 
-        units = [(c, t) for c in range(len(chunks)) for t in range(PACK)]
-        for u, (c, t) in enumerate(units):
-            fetch(c, t)
-            if u > 0:
-                gate(*units[u - 1])
-            subtract(c, t)
-            if c > 0 and t == 0:
-                interleave(c - 1)
-            if c > 0 and t == 1:
-                multiply(c - 1)
-        gate(*units[-1])
-        interleave(len(chunks) - 1)
-        multiply(len(chunks) - 1)
+        count = len(UNITS)
+        closing = [u for u in range(count) if UNITS[u][0] == PACK - 1]
+        for u in range(count + 2):
+            if u < count:
+                fetch(u)
+            if 0 <= u - 1 < count:
+                gate(u - 1)
+            if u - 2 in closing:
+                multiply(u - 2)
+            if u < count:
+                subtract(u)
+            if u - 1 in closing:
+                interleave(u - 1)
 
         h = [sb([P, S], F32, "h%d" % t) for t in range(PACK)]
         hop = [sb([P, S], F32, "hop%d" % t) for t in range(PACK)]
@@ -223,12 +257,12 @@ def tile_picked_hmixghardhopmx_none_po_kernel(
         out_words = out_1[0].rearrange("p n r -> p (n r)").bitcast(I32)
         for c, (j0, w) in enumerate(spans(OUT_CHUNKS)):
             cols = slice(j0, j0 + w)
-            far = sb([P, PACK, w], F32, "far%d" % c)
             res = sb([P, PACK, w], F32, "res%d" % c)
             ri = sb([P, w, PACK], BF16, "ri%d" % c)
             for t in range(PACK):
-                nc.scalar.activation(far[:, t], st[t][:].indirect(n3_t[:, j0 // 16 : (j0 + w) // 16]), ACT.Copy)
-                nc.vector.tensor_tensor(res[:, t], st[t][:, cols], far[:, t], ALU.max)
+                far = ring.tile([P, w], F32, name="far", bufs=3, align_bytes=64)
+                nc.scalar.activation(far[:], st[t][:].indirect(n3_t[:, j0 // 16 : (j0 + w) // 16]), ACT.Copy)
+                nc.vector.tensor_tensor(res[:, t], st[t][:, cols], far[:], ALU.max)
             nc.sync.dma_start(out=out_rows[:, :, cols], in_=res[:])
             nc.vector.tensor_copy(
                 out=ri[:].rearrange("p (c i) t -> p c t i", i=4), in_=res[:].rearrange("p t (c i) -> p c t i", i=4)

@@ -65,12 +65,11 @@ def tile_picked_hmixghardhopmx_none_po_kernel(
         def load_scales(queue, scales, raw):
             for q in range(4):
                 rows = scales[0][4 * q : 4 * q + 4, :].bitcast(I32)
-                queue.dma_start(out=raw[32 * q : 32 * q + 32, :].bitcast(I32), in_=rows.unsqueeze(0).to_broadcast([8, 4, S // 4]))
+                queue[q % 2].dma_start(out=raw[32 * q : 32 * q + 32, :].bitcast(I32), in_=rows.unsqueeze(0).to_broadcast([8, 4, S // 4]))
 
-        def deal_words(engine, raw, name):
-            words = sb([P, 2 * S], U8, name)
+        def deal_words(engine, raw, words):
             engine.tensor_copy(
-                out=words[:].rearrange("p (t m b) -> p t b m", t=PACK, b=2),
+                out=words.rearrange("p (t m b) -> p t b m", t=PACK, b=2),
                 in_=raw.rearrange("p (m t b) -> p t b m", t=PACK, b=2),
             )
             return words
@@ -94,8 +93,8 @@ def tile_picked_hmixghardhopmx_none_po_kernel(
             placed = sb([P, S], U8, name + "_placed")
             nc.vector.tensor_copy(out=got[:], in_=xs[:].indirect(lists[:]))
             nc.vector.tensor_copy(out=placed[:].bitcast(I32), in_=got[:].bitcast(I32))
-            for b in range(2):
-                queue[b].dma_start(out=placed[2 + b : P : 32, :].bitcast(I32), in_=got[16 + b : P : 32, :].bitcast(I32))
+            for r in range(1, 4):
+                queue.dma_start(out=placed[r:P:32, :].bitcast(I32), in_=got[8 * r : P : 32, :].bitcast(I32))
             return placed
 
         def pick_words(lists, name):
@@ -107,43 +106,40 @@ def tile_picked_hmixghardhopmx_none_po_kernel(
         warm = sb([P, 2], F32, "warm")
         nc.vector.memset(warm[:, 0:1], 0.0)
 
-        def load_token_scales(queue, b):
-            rows = x_scales[0][b:16:2, :].bitcast(I32)
-            queue.dma_start(out=xs[b:P:2, :].bitcast(I32), in_=rows.unsqueeze(1).to_broadcast([8, 8, T // 4]))
-
         nc.sync.dma_start(out=offs_t[:], in_=offs)
-        load_token_scales(nc.scalar, 1)
-        load_token_scales(nc.sync, 0)
-        raw_w1 = sb([P, 2 * S], U8, "raw_w")
-        load_words(nc.scalar, w1_words, raw_w1[:])
+        nc.scalar.dma_start(out=xs[:].bitcast(I32), in_=x_scales[0].bitcast(I32).unsqueeze(1).to_broadcast([16, 8, T // 4]))
         nc.sync.dma_start(out=two_t[:], in_=two)
-        nc.sync.dma_start(out=n1_t[:], in_=n1)
-        nc.sync.dma_start(out=n2_t[:], in_=n2)
-        nc.sync.dma_start(out=xw[:].bitcast(I32), in_=x_words[0].rearrange("p n r -> p (n r)").bitcast(I32))
         raw_s1 = sb([P, S], U8, "raw_s1")
-        load_scales(nc.sync, w1_scales, raw_s1[:])
-        nc.gpsimd.dma_start(out=gain[:], in_=gn.rearrange("(p t) o -> p (t o)", t=PACK))
+        load_scales((nc.scalar, nc.sync), w1_scales, raw_s1[:])
+        nc.sync.dma_start(out=xw[:].bitcast(I32), in_=x_words[0].rearrange("p n r -> p (n r)").bitcast(I32))
+        raw_w1 = sb([P, 2 * S], U8, "raw_w")
+        load_words(nc.gpsimd, w1_words, raw_w1[:])
+        raw_w32 = sb([P, 4 * S], U8, "raw_w32")
+        load_words(nc.gpsimd, w3_words, raw_w32[:, : 2 * S])
+        load_words(nc.gpsimd, w2_words, raw_w32[:, 2 * S :])
         nc.scalar.activation(warm[:, 1:2], warm[:, 0:1], ACT.Sigmoid)
         for t in range(PACK):
             nc.vector.memset(y[t][:, S:], 0.0)
 
-        xq_s = pick_scales(offs_t, "xq_s", (nc.scalar, nc.scalar), "xq_s_got")
+        xq_s = pick_scales(offs_t, "xq_s", nc.scalar, "xq_s_got")
+        nc.sync.dma_start(out=n1_t[:], in_=n1)
+        nc.sync.dma_start(out=n2_t[:], in_=n2)
         nc.sync.dma_start(out=n3_t[:], in_=n3)
-        w1_w = deal_words(nc.gpsimd, raw_w1[:], "w1_w")
-        x2_s = pick_scales(two_t, "x2_s", (nc.sync, nc.sync), "x2_s_got")
+        nc.sync.dma_start(out=gain[:], in_=gn.rearrange("(p t) o -> p (t o)", t=PACK))
+        w1_s = deal_scales(nc.gpsimd, raw_s1[:], "w1_s")
+        w1_t = sb([P, 2 * S], U8, "w1_t")
+        w1_w = deal_words(nc.gpsimd, raw_w1[:], w1_t[:])
+        x2_s = pick_scales(two_t, "x2_s", nc.sync, "x2_s_got")
         xq_w = sb([P, S], U32, "xq_w")
         for j0 in range(0, S, HALF):
             nc.vector.tensor_copy(out=xq_w[:, j0 : j0 + HALF], in_=xw[:].indirect(offs_t[:, j0 // 16 : (j0 + HALF) // 16]))
-        w1 = (w1_w, deal_scales(nc.gpsimd, raw_s1[:], "w1_s"))
-        raw_32 = sb([P, 6 * S], U8, "raw_w")
-        raw_w32 = raw_32[:, : 4 * S]
-        raw_s32 = raw_32[:, 4 * S :]
-        load_words(nc.sync, w3_words, raw_w32[:, : 2 * S])
-        load_words(nc.sync, w2_words, raw_w32[:, 2 * S :])
-        load_scales(nc.sync, w3_scales, raw_s32[:, :S])
-        load_scales(nc.sync, w2_scales, raw_s32[:, S:])
-        w3_w = deal_words(nc.gpsimd, raw_w32[:, : 2 * S], "w3_w")
-        w2_w = deal_words(nc.gpsimd, raw_w32[:, 2 * S :], "w2_w")
+        w1 = (w1_w, w1_s)
+        raw_s32 = sb([P, 2 * S], U8, "raw_w")
+        load_scales((nc.sync, nc.sync), w3_scales, raw_s32[:, :S])
+        load_scales((nc.sync, nc.sync), w2_scales, raw_s32[:, S:])
+        w32_t = sb([P, 4 * S], U8, "raw_s1")
+        w3_w = deal_words(nc.gpsimd, raw_w32[:, : 2 * S], w32_t[:, : 2 * S])
+        w2_w = deal_words(nc.gpsimd, raw_w32[:, 2 * S :], w32_t[:, 2 * S :])
 
         y_ps = [psum.tile([P, S], F32, name="y_ps%d" % t) for t in range(PACK)]
         first = psum.tile([P, HALF], F32, name="h_ps3")
@@ -162,10 +158,15 @@ def tile_picked_hmixghardhopmx_none_po_kernel(
         for t in range(PACK):
             if t not in Y_ON_SCALAR:
                 nc.vector.tensor_copy(out=y[t][:, :S], in_=y_ps[t][:])
-        w3 = (w3_w, deal_scales(nc.vector, raw_s32[:, :S], "w3_s"))
-        for t in range(PACK):
-            nc.tensor.matmul_mx(out=h_ps[t][:], rhs=x2_w[:].bitcast(FP8X4), rhs_scale=x2_s[:], start=True, stop=False, **stationary(w3, t))
-        w2 = (w2_w, deal_scales(nc.vector, raw_s32[:, S:], "w2_s"))
+        w3 = (w3_w, deal_scales(nc.gpsimd, raw_s32[:, :S], "w3_s"))
+        h_late = [psum.tile([P, S], F32, name="y_ps%d" % t) for t in range(PACK)]
+        for banks, cols in ((h_ps, slice(0, HALF)), (h_late, slice(HALF, S))):
+            for t in range(PACK):
+                nc.tensor.matmul_mx(
+                    out=banks[t][:, cols], rhs=x2_w[:, cols].bitcast(FP8X4), rhs_scale=x2_s[:, cols], start=True, stop=False,
+                    **stationary(w3, t)
+                )
+        w2 = (w2_w, deal_scales(nc.gpsimd, raw_s32[:, S:], "w2_s"))
 
         z_codes = sb([P, S], U32, "z_codes")
         z_scales = sb([P, S], U8, "z_scales")
@@ -179,9 +180,9 @@ def tile_picked_hmixghardhopmx_none_po_kernel(
             t, j0, w = UNITS[u]
             if j0 == 0 and t > 0 and t in Y_ON_SCALAR:
                 nc.scalar.copy(out=y[t][:, :S], in_=y_ps[t][:])
-            unit = ring.tile([P, 3 * w], F32, name="unit", align_bytes=64)
-            pairs = unit[:, : 2 * w]
-            mx = unit[:, 2 * w :]
+            pairs = ring.tile([P, 2 * w], F32, name="pairs", align_bytes=64)
+            top = sb([P, w], F32, "mx%d" % u)
+            mx = top[:]
             mn[u] = sb([P, w], F32, "mn%d" % u)
             sg[u] = sb([P, w], F32, "sg%d" % u)
             step = min(w, GATHER)
@@ -218,8 +219,8 @@ def tile_picked_hmixghardhopmx_none_po_kernel(
             )
             for m in range(PACK):
                 nc.tensor.matmul_mx(
-                    out=h_ps[m][:, cols], rhs=z_codes[:, cols].bitcast(FP8X4), rhs_scale=z_scales[:, cols],
-                    start=False, stop=(u == len(UNITS) - 1), **stationary(w2, m)
+                    out=(h_ps if j0 < HALF else h_late)[m][:, cols], rhs=z_codes[:, cols].bitcast(FP8X4), rhs_scale=z_scales[:, cols],
+                    start=False, stop=((j0 + w) % HALF == 0), **stationary(w2, m)
                 )
 
         count = len(UNITS)
@@ -236,14 +237,16 @@ def tile_picked_hmixghardhopmx_none_po_kernel(
             if u - 1 in closing:
                 interleave(u - 1)
 
-        h = [sb([P, S], F32, "h%d" % t) for t in range(PACK)]
+        h = [sb([P, S], F32, "y%d" % t) for t in range(PACK)]
+        for t in range(PACK):
+            nc.scalar.copy(out=h[t][:, :HALF], in_=h_ps[t][:, :HALF])
         hop = [sb([P, S], F32, "hop%d" % t) for t in range(PACK)]
         st = [sb([P, S], F32, "st%d" % t) for t in range(PACK)]
         for t in range(PACK):
             if t == 0:
-                nc.scalar.copy(out=h[t][:], in_=h_ps[t][:])
+                nc.scalar.copy(out=h[t][:, HALF:], in_=h_late[t][:, HALF:])
             else:
-                nc.vector.tensor_copy(out=h[t][:], in_=h_ps[t][:])
+                nc.vector.tensor_copy(out=h[t][:, HALF:], in_=h_late[t][:, HALF:])
         for t in range(PACK):
             for j0 in range(0, S, HALF):
                 nc.scalar.activation(
@@ -260,7 +263,7 @@ def tile_picked_hmixghardhopmx_none_po_kernel(
             res = sb([P, PACK, w], F32, "res%d" % c)
             ri = sb([P, w, PACK], BF16, "ri%d" % c)
             for t in range(PACK):
-                far = ring.tile([P, w], F32, name="far", bufs=3, align_bytes=64)
+                far = ring.tile([P, w], F32, name="far", bufs=4, align_bytes=64)
                 nc.scalar.activation(far[:], st[t][:].indirect(n3_t[:, j0 // 16 : (j0 + w) // 16]), ACT.Copy)
                 nc.vector.tensor_tensor(res[:, t], st[t][:, cols], far[:], ALU.max)
             nc.sync.dma_start(out=out_rows[:, :, cols], in_=res[:])

@@ -15,26 +15,22 @@ ACT = mybir.ActivationFunctionType
 
 P = 128
 PACK = 4
+QUADS = 4
+GROUP = 16
 T = 2048
 S = 512
+HALF = S // 2
+QUARTER = S // 4
 FLOPS = 3 * 2 * 512 * 512 * 512
 
-UNITS = ((0, 0, 256), (1, 0, 256), (2, 0, 256), (3, 0, 256), (0, 256, 256), (1, 256, 256), (2, 256, 256), (3, 256, 128), (3, 384, 128))
-GATHER = 256
-OUT_CHUNKS = (256, 128, 128)
-HALF = 256
-PAD = 16
-RING = 2
-Y_ON_SCALAR = (0,)
-
-
-def spans(widths):
-    out = []
-    start = 0
-    for w in widths:
-        out.append((start, w))
-        start = start + w
-    return out
+PIECES = (
+    [(t, 0, HALF) for t in range(PACK)]
+    + [(t, HALF, HALF) for t in range(PACK - 1)]
+    + [(PACK - 1, HALF, QUARTER), (PACK - 1, HALF + QUARTER, QUARTER)]
+)
+OUT_CHUNKS = ((0, HALF), (HALF, QUARTER), (HALF + QUARTER, QUARTER))
+PAIR_BUFS = 2
+FAR_BUFS = PACK
 
 
 def tile_picked_hmixghardhopmx_none_po_kernel(
@@ -44,31 +40,39 @@ def tile_picked_hmixghardhopmx_none_po_kernel(
     nc = tc.nc
     with ExitStack() as ctx:
         keep = ctx.enter_context(tc.tile_pool(name="keep", bufs=1))
-        ring = ctx.enter_context(tc.tile_pool(name="ring", bufs=RING))
+        ring = ctx.enter_context(tc.tile_pool(name="ring", bufs=PAIR_BUFS))
         psum = ctx.enter_context(tc.psum_pool(name="psum", bufs=1))
 
-        def sb(shape, dtype, name):
-            return keep.tile(shape, dtype, name=name, align_bytes=64)
+        def sb(shape, dtype, name, shares=None):
+            return keep.tile(shape, dtype, name=name, tag=shares or name, align_bytes=64)
 
-        offs_t = sb([P, 32], U16, "offs_t")
-        n1_t = sb([P, 64], U16, "n1_t")
-        two_t = sb([P, 32], U16, "two_t")
-        n2_t = sb([P, 32], U16, "n2_t")
-        n3_t = sb([P, 32], U16, "n3_t")
-        xw = sb([P, T], U32, "xw")
-        xs = sb([P, T], U8, "xs")
+        def bank(width, name, number):
+            return psum.tile([P, width], F32, name=name, tag="bank%d" % number)
+
+        def entries(lists, first, count):
+            return lists[:, first // GROUP : (first + count) // GROUP]
+
+        offs_t = sb([P, S // GROUP], U16, "offs_t")
+        n1_t = sb([P, 2 * S // GROUP], U16, "n1_t")
+        two_t = sb([P, S // GROUP], U16, "two_t")
+        n2_t = sb([P, S // GROUP], U16, "n2_t")
+        n3_t = sb([P, S // GROUP], U16, "n3_t")
+        table_words = sb([P, T], U32, "table_words")
+        table_scales = sb([P, T], U8, "table_scales")
         gain = sb([P, PACK], F32, "gain")
 
-        def load_words(queue, words, raw):
-            queue.dma_start(out=raw.bitcast(I32), in_=words[0].bitcast(I32))
+        def load_words(words, raw):
+            nc.gpsimd.dma_start(out=raw.bitcast(I32), in_=words[0].bitcast(I32))
 
-        def load_scales(queue, scales, raw):
-            for q in range(4):
+        def load_scales(queues, scales, raw):
+            for q in range(QUADS):
                 rows = scales[0][4 * q : 4 * q + 4, :].bitcast(I32)
-                queue[q % 2].dma_start(out=raw[32 * q : 32 * q + 32, :].bitcast(I32), in_=rows.unsqueeze(0).to_broadcast([8, 4, S // 4]))
+                queues[q % 2].dma_start(
+                    out=raw[32 * q : 32 * q + 32, :].bitcast(I32), in_=rows.unsqueeze(0).to_broadcast([8, 4, S // 4])
+                )
 
-        def deal_words(engine, raw, words):
-            engine.tensor_copy(
+        def deal_words(raw, words):
+            nc.gpsimd.tensor_copy(
                 out=words.rearrange("p (t m b) -> p t b m", t=PACK, b=2),
                 in_=raw.rearrange("p (m t b) -> p t b m", t=PACK, b=2),
             )
@@ -81,150 +85,143 @@ def tile_picked_hmixghardhopmx_none_po_kernel(
             )
             return scales
 
-        def stationary(weight, t):
-            words, scales = weight
-            return dict(
-                lhsT=words[:, 2 * P * t : 2 * P * (t + 1)].bitcast(FP4X4),
-                lhsT_scale=scales[:, P * t : P * (t + 1)],
+        def product(out, weight, t, codes, scales, cols, start, stop):
+            w_words, w_scales = weight
+            nc.tensor.matmul_mx(
+                out=out,
+                lhsT=w_words[:, 2 * P * t : 2 * P * (t + 1)].bitcast(FP4X4),
+                lhsT_scale=w_scales[:, P * t : P * (t + 1)],
+                rhs=codes[:, cols].bitcast(FP8X4),
+                rhs_scale=scales[:, cols],
+                start=start,
+                stop=stop,
             )
 
-        def pick_scales(lists, name, queue, stage):
-            got = sb([P, S], U8, stage)
-            placed = sb([P, S], U8, name + "_placed")
-            nc.vector.tensor_copy(out=got[:], in_=xs[:].indirect(lists[:]))
+        def pick_scales(lists, name, queue):
+            got = sb([P, S], U8, name + "_got")
+            placed = sb([P, S], U8, name)
+            nc.vector.tensor_copy(out=got[:], in_=table_scales[:].indirect(lists[:]))
             nc.vector.tensor_copy(out=placed[:].bitcast(I32), in_=got[:].bitcast(I32))
             for r in range(1, 4):
                 queue.dma_start(out=placed[r:P:32, :].bitcast(I32), in_=got[8 * r : P : 32, :].bitcast(I32))
             return placed
 
-        def pick_words(lists, name):
-            got = sb([P, S], U32, name)
-            nc.vector.tensor_copy(out=got[:], in_=xw[:].indirect(lists[:]))
-            return got
+        def interleave(out, rows):
+            nc.vector.tensor_copy(
+                out=out.rearrange("p (c i) t -> p c t i", i=4), in_=rows.rearrange("p t (c i) -> p c t i", i=4)
+            )
 
-        y = [sb([P, S + PAD], F32, "y%d" % t) for t in range(PACK)]
-        warm = sb([P, 2], F32, "warm")
-        nc.vector.memset(warm[:, 0:1], 0.0)
+        def quantise(codes, scales, cols, values):
+            nc.vector.quantize_mx(
+                out=codes[:, cols].bitcast(FP8X4), scales=scales[:, cols], in_=values.rearrange("p j t -> p (j t)")
+            )
+
+        window = [sb([P, 2 * S], F32, "window%d" % t) for t in range(PACK)]
 
         nc.sync.dma_start(out=offs_t[:], in_=offs)
-        nc.scalar.dma_start(out=xs[:].bitcast(I32), in_=x_scales[0].bitcast(I32).unsqueeze(1).to_broadcast([16, 8, T // 4]))
+        nc.scalar.dma_start(
+            out=table_scales[:].bitcast(I32), in_=x_scales[0].bitcast(I32).unsqueeze(1).to_broadcast([16, 8, T // 4])
+        )
         nc.sync.dma_start(out=two_t[:], in_=two)
         raw_s1 = sb([P, S], U8, "raw_s1")
         load_scales((nc.scalar, nc.sync), w1_scales, raw_s1[:])
-        nc.sync.dma_start(out=xw[:].bitcast(I32), in_=x_words[0].rearrange("p n r -> p (n r)").bitcast(I32))
-        raw_w1 = sb([P, 2 * S], U8, "raw_w")
-        load_words(nc.gpsimd, w1_words, raw_w1[:])
+        nc.sync.dma_start(out=table_words[:].bitcast(I32), in_=x_words[0].rearrange("p n r -> p (n r)").bitcast(I32))
+        raw_w1 = sb([P, 2 * S], U8, "raw_w1")
+        load_words(w1_words, raw_w1[:])
         raw_w32 = sb([P, 4 * S], U8, "raw_w32")
-        load_words(nc.gpsimd, w3_words, raw_w32[:, : 2 * S])
-        load_words(nc.gpsimd, w2_words, raw_w32[:, 2 * S :])
-        nc.scalar.activation(warm[:, 1:2], warm[:, 0:1], ACT.Sigmoid)
+        load_words(w3_words, raw_w32[:, : 2 * S])
+        load_words(w2_words, raw_w32[:, 2 * S :])
         for t in range(PACK):
-            nc.vector.memset(y[t][:, S:], 0.0)
+            nc.vector.memset(window[t][:, S:], 0.0)
+        warm = sb([P, 1], F32, "warm")
+        nc.scalar.activation(warm[:], window[0][:, S : S + 1], ACT.Sigmoid)
 
-        xq_s = pick_scales(offs_t, "xq_s", nc.scalar, "xq_s_got")
+        hashed_scales = pick_scales(offs_t, "hashed_scales", nc.scalar)
         nc.sync.dma_start(out=n1_t[:], in_=n1)
         nc.sync.dma_start(out=n2_t[:], in_=n2)
         nc.sync.dma_start(out=n3_t[:], in_=n3)
         nc.sync.dma_start(out=gain[:], in_=gn.rearrange("(p t) o -> p (t o)", t=PACK))
         w1_s = deal_scales(nc.gpsimd, raw_s1[:], "w1_s")
-        w1_t = sb([P, 2 * S], U8, "w1_t")
-        w1_w = deal_words(nc.gpsimd, raw_w1[:], w1_t[:])
-        x2_s = pick_scales(two_t, "x2_s", nc.sync, "x2_s_got")
-        xq_w = sb([P, S], U32, "xq_w")
-        for j0 in range(0, S, HALF):
-            nc.vector.tensor_copy(out=xq_w[:, j0 : j0 + HALF], in_=xw[:].indirect(offs_t[:, j0 // 16 : (j0 + HALF) // 16]))
-        w1 = (w1_w, w1_s)
-        raw_s32 = sb([P, 2 * S], U8, "raw_w")
+        w1_w = sb([P, 2 * S], U8, "w1_w", shares="raw_s1")
+        w1 = (deal_words(raw_w1[:], w1_w[:]), w1_s)
+        plain_scales = pick_scales(two_t, "plain_scales", nc.sync)
+        hashed_words = sb([P, S], U32, "hashed_words")
+        for j0 in (0, HALF):
+            nc.vector.tensor_copy(out=hashed_words[:, j0 : j0 + HALF], in_=table_words[:].indirect(entries(offs_t, j0, HALF)))
+        raw_s32 = sb([P, 2 * S], U8, "raw_s32", shares="hashed_scales_got")
         load_scales((nc.sync, nc.sync), w3_scales, raw_s32[:, :S])
         load_scales((nc.sync, nc.sync), w2_scales, raw_s32[:, S:])
-        w32_t = sb([P, 4 * S], U8, "raw_s1")
-        w3_w = deal_words(nc.gpsimd, raw_w32[:, : 2 * S], w32_t[:, : 2 * S])
-        w2_w = deal_words(nc.gpsimd, raw_w32[:, 2 * S :], w32_t[:, 2 * S :])
+        w32_w = sb([P, 4 * S], U8, "w32_w", shares="raw_w1")
+        w3_w = deal_words(raw_w32[:, : 2 * S], w32_w[:, : 2 * S])
+        w2_w = deal_words(raw_w32[:, 2 * S :], w32_w[:, 2 * S :])
 
-        y_ps = [psum.tile([P, S], F32, name="y_ps%d" % t) for t in range(PACK)]
-        first = psum.tile([P, HALF], F32, name="h_ps3")
-        nc.tensor.matmul_mx(
-            out=first[:], rhs=xq_w[:, :HALF].bitcast(FP8X4), rhs_scale=xq_s[:, :HALF], start=True, stop=True, **stationary(w1, 0)
-        )
-        nc.scalar.copy(out=y[0][:, :HALF], in_=first[:])
-        nc.tensor.matmul_mx(
-            out=y_ps[0][:, HALF:], rhs=xq_w[:, HALF:].bitcast(FP8X4), rhs_scale=xq_s[:, HALF:], start=True, stop=True, **stationary(w1, 0)
-        )
-        nc.scalar.copy(out=y[0][:, HALF:S], in_=y_ps[0][:, HALF:])
+        left, right, whole = slice(0, HALF), slice(HALF, S), slice(0, S)
+        y_ps = [bank(S, "y_ps%d" % t, t) for t in range(PACK)]
+        y0_left = bank(HALF, "y0_left", 2 * PACK - 1)
+        product(y0_left[:], w1, 0, hashed_words, hashed_scales, left, True, True)
+        nc.scalar.copy(out=window[0][:, left], in_=y0_left[:])
+        product(y_ps[0][:, right], w1, 0, hashed_words, hashed_scales, right, True, True)
+        nc.scalar.copy(out=window[0][:, right], in_=y_ps[0][:, right])
         for t in range(1, PACK):
-            nc.tensor.matmul_mx(out=y_ps[t][:], rhs=xq_w[:].bitcast(FP8X4), rhs_scale=xq_s[:], start=True, stop=True, **stationary(w1, t))
-        h_ps = [psum.tile([P, S], F32, name="h_ps%d" % t) for t in range(PACK)]
-        x2_w = pick_words(two_t, "x2_w")
-        for t in range(PACK):
-            if t not in Y_ON_SCALAR:
-                nc.vector.tensor_copy(out=y[t][:, :S], in_=y_ps[t][:])
-        w3 = (w3_w, deal_scales(nc.gpsimd, raw_s32[:, :S], "w3_s"))
-        h_late = [psum.tile([P, S], F32, name="y_ps%d" % t) for t in range(PACK)]
-        for banks, cols in ((h_ps, slice(0, HALF)), (h_late, slice(HALF, S))):
+            product(y_ps[t][:], w1, t, hashed_words, hashed_scales, whole, True, True)
+        plain_words = sb([P, S], U32, "plain_words")
+        nc.vector.tensor_copy(out=plain_words[:], in_=table_words[:].indirect(two_t[:]))
+        for t in range(1, PACK):
+            nc.vector.tensor_copy(out=window[t][:, whole], in_=y_ps[t][:])
+
+        w3 = (w3_w, deal_scales(nc.vector, raw_s32[:, :S], "w3_s"))
+        h_left = [bank(S, "h_left%d" % t, PACK + t) for t in range(PACK)]
+        h_right = [bank(S, "h_right%d" % t, t) for t in range(PACK)]
+        for banks, cols in ((h_left, left), (h_right, right)):
             for t in range(PACK):
-                nc.tensor.matmul_mx(
-                    out=banks[t][:, cols], rhs=x2_w[:, cols].bitcast(FP8X4), rhs_scale=x2_s[:, cols], start=True, stop=False,
-                    **stationary(w3, t)
-                )
-        w2 = (w2_w, deal_scales(nc.gpsimd, raw_s32[:, S:], "w2_s"))
+                product(banks[t][:, cols], w3, t, plain_words, plain_scales, cols, True, False)
+        w2 = (w2_w, deal_scales(nc.vector, raw_s32[:, S:], "w2_s"))
 
         z_codes = sb([P, S], U32, "z_codes")
         z_scales = sb([P, S], U8, "z_scales")
-        zt = sb([P, PACK, S], BF16, "zt")
-        mn = {}
-        sg = {}
-        df = {}
-        zi = {}
+        z_rows = sb([P, PACK, S], BF16, "z_rows")
+        smaller = {}
+        sigmoid = {}
+        diff = {}
+        z_side = {}
 
         def fetch(u):
-            t, j0, w = UNITS[u]
-            if j0 == 0 and t > 0 and t in Y_ON_SCALAR:
-                nc.scalar.copy(out=y[t][:, :S], in_=y_ps[t][:])
+            t, j0, w = PIECES[u]
             pairs = ring.tile([P, 2 * w], F32, name="pairs", align_bytes=64)
-            top = sb([P, w], F32, "mx%d" % u)
-            mx = top[:]
-            mn[u] = sb([P, w], F32, "mn%d" % u)
-            sg[u] = sb([P, w], F32, "sg%d" % u)
-            step = min(w, GATHER)
-            for a in range(0, w, step):
-                nc.scalar.activation(
-                    pairs[:, 2 * a : 2 * (a + step)], y[t][:].indirect(n1_t[:, (j0 + a) // 8 : (j0 + a + step) // 8]), ACT.Copy
-                )
-            nc.vector.tensor_tensor(mx, pairs[:, 0::2], pairs[:, 1::2], ALU.max)
-            nc.vector.tensor_tensor(mn[u][:], pairs[:, 0::2], pairs[:, 1::2], ALU.min)
-            nc.scalar.activation(sg[u][:], mx, ACT.Sigmoid)
+            larger = sb([P, w], F32, "larger%d" % u)
+            smaller[u] = sb([P, w], F32, "smaller%d" % u)
+            sigmoid[u] = sb([P, w], F32, "sigmoid%d" % u)
+            nc.scalar.activation(pairs[:], window[t][:].indirect(entries(n1_t, 2 * j0, 2 * w)), ACT.Copy)
+            nc.vector.tensor_tensor(larger[:], pairs[:, 0::2], pairs[:, 1::2], ALU.max)
+            nc.vector.tensor_tensor(smaller[u][:], pairs[:, 0::2], pairs[:, 1::2], ALU.min)
+            nc.scalar.activation(sigmoid[u][:], larger[:], ACT.Sigmoid)
 
         def subtract(u):
-            t, j0, w = UNITS[u]
-            df[u] = sb([P, w], F32, "df%d" % u)
-            nc.vector.tensor_tensor(df[u][:], y[t][:, j0 : j0 + w], mn[u][:], ALU.subtract)
+            t, j0, w = PIECES[u]
+            diff[u] = sb([P, w], F32, "diff%d" % u)
+            nc.vector.tensor_tensor(diff[u][:], window[t][:, j0 : j0 + w], smaller[u][:], ALU.subtract)
 
         def gate(u):
-            t, j0, w = UNITS[u]
-            nc.vector.scalar_tensor_tensor(zt[:, t, j0 : j0 + w], df[u][:], gain[:, t : t + 1], sg[u][:], ALU.mult, ALU.mult)
-
-        def interleave(u):
-            t, j0, w = UNITS[u]
-            zi[u] = sb([P, w, PACK], BF16, "zi%d" % u)
-            nc.vector.tensor_copy(
-                out=zi[u][:].rearrange("p (c i) t -> p c t i", i=4),
-                in_=zt[:, :, j0 : j0 + w].rearrange("p t (c i) -> p c t i", i=4),
+            t, j0, w = PIECES[u]
+            nc.vector.scalar_tensor_tensor(
+                z_rows[:, t, j0 : j0 + w], diff[u][:], gain[:, t : t + 1], sigmoid[u][:], ALU.mult, ALU.mult
             )
+
+        def regroup(u):
+            t, j0, w = PIECES[u]
+            z_side[u] = sb([P, w, PACK], BF16, "z_side%d" % u)
+            interleave(z_side[u][:], z_rows[:, :, j0 : j0 + w])
 
         def multiply(u):
-            t, j0, w = UNITS[u]
+            t, j0, w = PIECES[u]
             cols = slice(j0, j0 + w)
-            nc.vector.quantize_mx(
-                out=z_codes[:, cols].bitcast(FP8X4), scales=z_scales[:, cols], in_=zi[u][:].rearrange("p j t -> p (j t)")
-            )
+            quantise(z_codes, z_scales, cols, z_side[u][:])
+            banks = h_left if j0 < HALF else h_right
             for m in range(PACK):
-                nc.tensor.matmul_mx(
-                    out=(h_ps if j0 < HALF else h_late)[m][:, cols], rhs=z_codes[:, cols].bitcast(FP8X4), rhs_scale=z_scales[:, cols],
-                    start=False, stop=((j0 + w) % HALF == 0), **stationary(w2, m)
-                )
+                product(banks[m][:, cols], w2, m, z_codes, z_scales, cols, False, (j0 + w) % HALF == 0)
 
-        count = len(UNITS)
-        closing = [u for u in range(count) if UNITS[u][0] == PACK - 1]
+        count = len(PIECES)
+        closing = [u for u in range(count) if PIECES[u][0] == PACK - 1]
         for u in range(count + 2):
             if u < count:
                 fetch(u)
@@ -235,45 +232,38 @@ def tile_picked_hmixghardhopmx_none_po_kernel(
             if u < count:
                 subtract(u)
             if u - 1 in closing:
-                interleave(u - 1)
+                regroup(u - 1)
 
-        h = [sb([P, S], F32, "y%d" % t) for t in range(PACK)]
         for t in range(PACK):
-            nc.scalar.copy(out=h[t][:, :HALF], in_=h_ps[t][:, :HALF])
+            nc.scalar.copy(out=window[t][:, left], in_=h_left[t][:, left])
+        nc.scalar.copy(out=window[0][:, right], in_=h_right[0][:, right])
+        for t in range(1, PACK):
+            nc.vector.tensor_copy(out=window[t][:, right], in_=h_right[t][:, right])
         hop = [sb([P, S], F32, "hop%d" % t) for t in range(PACK)]
         st = [sb([P, S], F32, "st%d" % t) for t in range(PACK)]
         for t in range(PACK):
-            if t == 0:
-                nc.scalar.copy(out=h[t][:, HALF:], in_=h_late[t][:, HALF:])
-            else:
-                nc.vector.tensor_copy(out=h[t][:, HALF:], in_=h_late[t][:, HALF:])
-        for t in range(PACK):
-            for j0 in range(0, S, HALF):
-                nc.scalar.activation(
-                    hop[t][:, j0 : j0 + HALF], h[t][:].indirect(n2_t[:, j0 // 16 : (j0 + HALF) // 16]), ACT.Copy
-                )
-            nc.vector.tensor_tensor(st[t][:], h[t][:], hop[t][:], ALU.subtract)
+            nc.scalar.activation(hop[t][:], window[t][:].indirect(n2_t[:]), ACT.Copy)
+            nc.vector.tensor_tensor(st[t][:], window[t][:, whole], hop[t][:], ALU.subtract)
 
-        o_codes = sb([P, S], U32, "o_codes")
-        o_scales = sb([P, S], U8, "o_scales")
+        out_codes = sb([P, S], U32, "out_codes")
+        out_scales = sb([P, S], U8, "out_scales")
         out_rows = out_0.rearrange("(p t) j -> p t j", t=PACK)
         out_words = out_1[0].rearrange("p n r -> p (n r)").bitcast(I32)
-        for c, (j0, w) in enumerate(spans(OUT_CHUNKS)):
+        for c, (j0, w) in enumerate(OUT_CHUNKS):
             cols = slice(j0, j0 + w)
-            res = sb([P, PACK, w], F32, "res%d" % c)
-            ri = sb([P, w, PACK], BF16, "ri%d" % c)
+            result = sb([P, PACK, w], F32, "result%d" % c)
+            result_side = sb([P, w, PACK], BF16, "result_side%d" % c)
             for t in range(PACK):
-                far = ring.tile([P, w], F32, name="far", bufs=4, align_bytes=64)
-                nc.scalar.activation(far[:], st[t][:].indirect(n3_t[:, j0 // 16 : (j0 + w) // 16]), ACT.Copy)
-                nc.vector.tensor_tensor(res[:, t], st[t][:, cols], far[:], ALU.max)
-            nc.sync.dma_start(out=out_rows[:, :, cols], in_=res[:])
-            nc.vector.tensor_copy(
-                out=ri[:].rearrange("p (c i) t -> p c t i", i=4), in_=res[:].rearrange("p t (c i) -> p c t i", i=4)
-            )
-            nc.vector.quantize_mx(
-                out=o_codes[:, cols].bitcast(FP8X4), scales=o_scales[:, cols], in_=ri[:].rearrange("p j t -> p (j t)")
-            )
-            nc.sync.dma_start(out=out_words[:, cols], in_=o_codes[:, cols].bitcast(I32))
-        for q in range(4):
+                far = ring.tile([P, w], F32, name="far", bufs=FAR_BUFS, align_bytes=64)
+                nc.scalar.activation(far[:], st[t][:].indirect(entries(n3_t, j0, w)), ACT.Copy)
+                nc.vector.tensor_tensor(result[:, t], st[t][:, cols], far[:], ALU.max)
+            nc.sync.dma_start(out=out_rows[:, :, cols], in_=result[:])
+            interleave(result_side[:], result[:])
+            quantise(out_codes, out_scales, cols, result_side[:])
+            queue = nc.scalar if j0 + w == S else nc.sync
+            queue.dma_start(out=out_words[:, cols], in_=out_codes[:, cols].bitcast(I32))
+        for q in range(QUADS):
             queue = nc.scalar if q % 2 else nc.sync
-            queue.dma_start(out=out_2[0][4 * q : 4 * q + 4, :].bitcast(I32), in_=o_scales[32 * q : 32 * q + 4, :].bitcast(I32))
+            queue.dma_start(
+                out=out_2[0][4 * q : 4 * q + 4, :].bitcast(I32), in_=out_scales[32 * q : 32 * q + 4, :].bitcast(I32)
+            )

@@ -71,10 +71,10 @@ def tile_picked_hmixghardhopmx_none_po_kernel(
                     out=raw[32 * q : 32 * q + 32, :].bitcast(I32), in_=rows.unsqueeze(0).to_broadcast([8, 4, S // 4])
                 )
 
-        def deal_words(raw, words):
-            nc.gpsimd.tensor_copy(
-                out=words.rearrange("p (t m b) -> p t b m", t=PACK, b=2),
-                in_=raw.rearrange("p (m t b) -> p t b m", t=PACK, b=2),
+        def deal_words(engine, order, raw, words):
+            engine.tensor_copy(
+                out=words.rearrange("p (t m b) -> p " + order, t=PACK, b=2),
+                in_=raw.rearrange("p (m t b) -> p " + order, t=PACK, b=2),
             )
             return words
 
@@ -143,7 +143,7 @@ def tile_picked_hmixghardhopmx_none_po_kernel(
         nc.sync.dma_start(out=gain[:], in_=gn.rearrange("(p t) o -> p (t o)", t=PACK))
         w1_s = deal_scales(nc.gpsimd, raw_s1[:], "w1_s")
         w1_w = sb([P, 2 * S], U8, "w1_w", shares="raw_s1")
-        w1 = (deal_words(raw_w1[:], w1_w[:]), w1_s)
+        w1 = (deal_words(nc.gpsimd, "t b m", raw_w1[:], w1_w[:]), w1_s)
         plain_scales = pick_scales(two_t, "plain_scales", nc.sync)
         hashed_words = sb([P, S], U32, "hashed_words")
         for j0 in (0, HALF):
@@ -151,9 +151,8 @@ def tile_picked_hmixghardhopmx_none_po_kernel(
         raw_s32 = sb([P, 2 * S], U8, "raw_s32", shares="hashed_scales_got")
         load_scales((nc.sync, nc.sync), w3_scales, raw_s32[:, :S])
         load_scales((nc.sync, nc.sync), w2_scales, raw_s32[:, S:])
-        w32_w = sb([P, 4 * S], U8, "w32_w", shares="raw_w1")
-        w3_w = deal_words(raw_w32[:, : 2 * S], w32_w[:, : 2 * S])
-        w2_w = deal_words(raw_w32[:, 2 * S :], w32_w[:, 2 * S :])
+        w3_w = sb([P, 2 * S], U8, "w3_w", shares="raw_w1")
+        deal_words(nc.gpsimd, "t b m", raw_w32[:, : 2 * S], w3_w[:])
 
         left, right, whole = slice(0, HALF), slice(HALF, S), slice(0, S)
         y_ps = [bank(S, "y_ps%d" % t, t) for t in range(PACK)]
@@ -175,7 +174,8 @@ def tile_picked_hmixghardhopmx_none_po_kernel(
         for banks, cols in ((h_left, left), (h_right, right)):
             for t in range(PACK):
                 product(banks[t][:, cols], w3, t, plain_words, plain_scales, cols, True, False)
-        w2 = (w2_w, deal_scales(nc.vector, raw_s32[:, S:], "w2_s"))
+        w2_w = sb([P, 2 * S], U8, "w2_w", shares="plain_scales_got")
+        w2 = (deal_words(nc.vector, "t m b", raw_w32[:, 2 * S :], w2_w[:]), deal_scales(nc.vector, raw_s32[:, S:], "w2_s"))
 
         z_codes = sb([P, S], U32, "z_codes")
         z_scales = sb([P, S], U8, "z_scales")

from contextlib import ExitStack

import concourse.mybir as mybir

F32 = mybir.dt.float32
BF16 = mybir.dt.bfloat16
I32 = mybir.dt.int32
U32 = mybir.dt.uint32
U16 = mybir.dt.uint16
U8 = mybir.dt.uint8
FP8X4 = mybir.dt.float8_e4m3fn_x4
FP4X4 = mybir.dt.float4_e2m1fn_x4
ALU = mybir.AluOpType
ACT = mybir.ActivationFunctionType

P = 128
PACK = 4
QUADS = 4
GROUP = 16
T = 2048
S = 512
HALF = S // 2
QUARTER = S // 4
FLOPS = 3 * 2 * 512 * 512 * 512

PIECES = (
    [(t, 0, HALF) for t in range(PACK)]
    + [(t, HALF, HALF) for t in range(PACK - 1)]
    + [(PACK - 1, HALF, QUARTER), (PACK - 1, HALF + QUARTER, QUARTER)]
)
OUT_CHUNKS = ((0, HALF), (HALF, QUARTER), (HALF + QUARTER, QUARTER))
PAIR_BUFS = 2
FAR_BUFS = PACK


def tile_picked_hmixghardhopmx_none_po_kernel(
    tc, x_words, x_scales, w1_words, w1_scales, gn, w2_words, w2_scales, w3_words, w3_scales,
    offs, n1, two, n2, n3, out_0, out_1, out_2,
):
    nc = tc.nc
    with ExitStack() as ctx:
        keep = ctx.enter_context(tc.tile_pool(name="keep", bufs=1))
        ring = ctx.enter_context(tc.tile_pool(name="ring", bufs=PAIR_BUFS))
        psum = ctx.enter_context(tc.psum_pool(name="psum", bufs=1))

        def sb(shape, dtype, name, shares=None):
            return keep.tile(shape, dtype, name=name, tag=shares or name, align_bytes=64)

        def bank(width, name, number):
            return psum.tile([P, width], F32, name=name, tag="bank%d" % number)

        def entries(lists, first, count):
            return lists[:, first // GROUP : (first + count) // GROUP]

        offs_t = sb([P, S // GROUP], U16, "offs_t")
        n1_t = sb([P, 2 * S // GROUP], U16, "n1_t")
        two_t = sb([P, S // GROUP], U16, "two_t")
        n2_t = sb([P, S // GROUP], U16, "n2_t")
        n3_t = sb([P, S // GROUP], U16, "n3_t")
        table_words = sb([P, T], U32, "table_words")
        table_scales = sb([P, T], U8, "table_scales")
        gain = sb([P, PACK], F32, "gain")

        def load_words(words, raw):
            nc.gpsimd.dma_start(out=raw.bitcast(I32), in_=words[0].bitcast(I32))

        def load_scales(queues, scales, raw):
            for q in range(QUADS):
                rows = scales[0][4 * q : 4 * q + 4, :].bitcast(I32)
                queues[q % 2].dma_start(
                    out=raw[32 * q : 32 * q + 32, :].bitcast(I32), in_=rows.unsqueeze(0).to_broadcast([8, 4, S // 4])
                )

        def deal_words(engine, order, raw, words):
            engine.tensor_copy(
                out=words.rearrange("p (t m b) -> p " + order, t=PACK, b=2),
                in_=raw.rearrange("p (m t b) -> p " + order, t=PACK, b=2),
            )
            return words

        def deal_scales(engine, raw, name):
            scales = sb([P, S], U8, name)
            engine.tensor_copy(
                out=scales[:].rearrange("p (t m) -> p t m", t=PACK), in_=raw.rearrange("p (m t) -> p t m", t=PACK)
            )
            return scales

        def product(out, weight, t, codes, scales, cols, start, stop):
            w_words, w_scales = weight
            nc.tensor.matmul_mx(
                out=out,
                lhsT=w_words[:, 2 * P * t : 2 * P * (t + 1)].bitcast(FP4X4),
                lhsT_scale=w_scales[:, P * t : P * (t + 1)],
                rhs=codes[:, cols].bitcast(FP8X4),
                rhs_scale=scales[:, cols],
                start=start,
                stop=stop,
            )

        def pick_scales(lists, name, queue):
            got = sb([P, S], U8, name + "_got")
            placed = sb([P, S], U8, name)
            nc.vector.tensor_copy(out=got[:], in_=table_scales[:].indirect(lists[:]))
            nc.vector.tensor_copy(out=placed[:].bitcast(I32), in_=got[:].bitcast(I32))
            for r in range(1, 4):
                queue.dma_start(out=placed[r:P:32, :].bitcast(I32), in_=got[8 * r : P : 32, :].bitcast(I32))
            return placed

        def interleave(out, rows):
            nc.vector.tensor_copy(
                out=out.rearrange("p (c i) t -> p c t i", i=4), in_=rows.rearrange("p t (c i) -> p c t i", i=4)
            )

        def quantise(codes, scales, cols, values):
            nc.vector.quantize_mx(
                out=codes[:, cols].bitcast(FP8X4), scales=scales[:, cols], in_=values.rearrange("p j t -> p (j t)")
            )

        window = [sb([P, 2 * S], F32, "window%d" % t) for t in range(PACK)]

        nc.sync.dma_start(out=offs_t[:], in_=offs)
        nc.scalar.dma_start(
            out=table_scales[:].bitcast(I32), in_=x_scales[0].bitcast(I32).unsqueeze(1).to_broadcast([16, 8, T // 4])
        )
        nc.sync.dma_start(out=two_t[:], in_=two)
        raw_s1 = sb([P, S], U8, "raw_s1")
        load_scales((nc.scalar, nc.sync), w1_scales, raw_s1[:])
        nc.sync.dma_start(out=table_words[:].bitcast(I32), in_=x_words[0].rearrange("p n r -> p (n r)").bitcast(I32))
        raw_w1 = sb([P, 2 * S], U8, "raw_w1")
        load_words(w1_words, raw_w1[:])
        raw_w32 = sb([P, 4 * S], U8, "raw_w32")
        load_words(w3_words, raw_w32[:, : 2 * S])
        load_words(w2_words, raw_w32[:, 2 * S :])
        for t in range(PACK):
            nc.vector.memset(window[t][:, S:], 0.0)
        warm = sb([P, 1], F32, "warm")
        nc.scalar.activation(warm[:], window[0][:, S : S + 1], ACT.Sigmoid)

        hashed_scales = pick_scales(offs_t, "hashed_scales", nc.scalar)
        nc.sync.dma_start(out=n1_t[:], in_=n1)
        nc.sync.dma_start(out=n2_t[:], in_=n2)
        nc.sync.dma_start(out=n3_t[:], in_=n3)
        nc.sync.dma_start(out=gain[:], in_=gn.rearrange("(p t) o -> p (t o)", t=PACK))
        w1_s = deal_scales(nc.gpsimd, raw_s1[:], "w1_s")
        w1_w = sb([P, 2 * S], U8, "w1_w", shares="raw_s1")
        w1 = (deal_words(nc.gpsimd, "t b m", raw_w1[:], w1_w[:]), w1_s)
        plain_scales = pick_scales(two_t, "plain_scales", nc.sync)
        hashed_words = sb([P, S], U32, "hashed_words")
        for j0 in (0, HALF):
            nc.vector.tensor_copy(out=hashed_words[:, j0 : j0 + HALF], in_=table_words[:].indirect(entries(offs_t, j0, HALF)))
        raw_s32 = sb([P, 2 * S], U8, "raw_s32", shares="hashed_scales_got")
        load_scales((nc.sync, nc.sync), w3_scales, raw_s32[:, :S])
        load_scales((nc.sync, nc.sync), w2_scales, raw_s32[:, S:])
        w3_w = sb([P, 2 * S], U8, "w3_w", shares="raw_w1")
        deal_words(nc.gpsimd, "t b m", raw_w32[:, : 2 * S], w3_w[:])

        left, right, whole = slice(0, HALF), slice(HALF, S), slice(0, S)
        y_ps = [bank(S, "y_ps%d" % t, t) for t in range(PACK)]
        y0_left = bank(HALF, "y0_left", 2 * PACK - 1)
        product(y0_left[:], w1, 0, hashed_words, hashed_scales, left, True, True)
        nc.scalar.copy(out=window[0][:, left], in_=y0_left[:])
        product(y_ps[0][:, right], w1, 0, hashed_words, hashed_scales, right, True, True)
        nc.scalar.copy(out=window[0][:, right], in_=y_ps[0][:, right])
        for t in range(1, PACK):
            product(y_ps[t][:], w1, t, hashed_words, hashed_scales, whole, True, True)
        plain_words = sb([P, S], U32, "plain_words")
        nc.vector.tensor_copy(out=plain_words[:], in_=table_words[:].indirect(two_t[:]))
        for t in range(1, PACK):
            nc.vector.tensor_copy(out=window[t][:, whole], in_=y_ps[t][:])

        w3 = (w3_w, deal_scales(nc.vector, raw_s32[:, :S], "w3_s"))
        h_left = [bank(S, "h_left%d" % t, PACK + t) for t in range(PACK)]
        h_right = [bank(S, "h_right%d" % t, t) for t in range(PACK)]
        for banks, cols in ((h_left, left), (h_right, right)):
            for t in range(PACK):
                product(banks[t][:, cols], w3, t, plain_words, plain_scales, cols, True, False)
        w2_w = sb([P, 2 * S], U8, "w2_w", shares="plain_scales_got")
        w2 = (deal_words(nc.vector, "t m b", raw_w32[:, 2 * S :], w2_w[:]), deal_scales(nc.vector, raw_s32[:, S:], "w2_s"))

        z_codes = sb([P, S], U32, "z_codes")
        z_scales = sb([P, S], U8, "z_scales")
        z_rows = sb([P, PACK, S], BF16, "z_rows")
        smaller = {}
        sigmoid = {}
        diff = {}
        z_side = {}

        def fetch(u):
            t, j0, w = PIECES[u]
            pairs = ring.tile([P, 2 * w], F32, name="pairs", align_bytes=64)
            larger = sb([P, w], F32, "larger%d" % u)
            smaller[u] = sb([P, w], F32, "smaller%d" % u)
            sigmoid[u] = sb([P, w], F32, "sigmoid%d" % u)
            nc.scalar.activation(pairs[:], window[t][:].indirect(entries(n1_t, 2 * j0, 2 * w)), ACT.Copy)
            nc.vector.tensor_tensor(larger[:], pairs[:, 0::2], pairs[:, 1::2], ALU.max)
            nc.vector.tensor_tensor(smaller[u][:], pairs[:, 0::2], pairs[:, 1::2], ALU.min)
            nc.scalar.activation(sigmoid[u][:], larger[:], ACT.Sigmoid)

        def subtract(u):
            t, j0, w = PIECES[u]
            diff[u] = sb([P, w], F32, "diff%d" % u)
            nc.vector.tensor_tensor(diff[u][:], window[t][:, j0 : j0 + w], smaller[u][:], ALU.subtract)

        def gate(u):
            t, j0, w = PIECES[u]
            nc.vector.scalar_tensor_tensor(
                z_rows[:, t, j0 : j0 + w], diff[u][:], gain[:, t : t + 1], sigmoid[u][:], ALU.mult, ALU.mult
            )

        def regroup(u):
            t, j0, w = PIECES[u]
            z_side[u] = sb([P, w, PACK], BF16, "z_side%d" % u)
            interleave(z_side[u][:], z_rows[:, :, j0 : j0 + w])

        def multiply(u):
            t, j0, w = PIECES[u]
            cols = slice(j0, j0 + w)
            quantise(z_codes, z_scales, cols, z_side[u][:])
            banks = h_left if j0 < HALF else h_right
            for m in range(PACK):
                product(banks[m][:, cols], w2, m, z_codes, z_scales, cols, False, (j0 + w) % HALF == 0)

        count = len(PIECES)
        closing = [u for u in range(count) if PIECES[u][0] == PACK - 1]
        for u in range(count + 2):
            if u < count:
                fetch(u)
            if 0 <= u - 1 < count:
                gate(u - 1)
            if u - 2 in closing:
                multiply(u - 2)
            if u < count:
                subtract(u)
            if u - 1 in closing:
                regroup(u - 1)

        for t in range(PACK):
            nc.scalar.copy(out=window[t][:, left], in_=h_left[t][:, left])
        nc.scalar.copy(out=window[0][:, right], in_=h_right[0][:, right])
        for t in range(1, PACK):
            nc.vector.tensor_copy(out=window[t][:, right], in_=h_right[t][:, right])
        hop = [sb([P, S], F32, "hop%d" % t) for t in range(PACK)]
        st = [sb([P, S], F32, "st%d" % t) for t in range(PACK)]
        for t in range(PACK):
            nc.scalar.activation(hop[t][:], window[t][:].indirect(n2_t[:]), ACT.Copy)
            nc.vector.tensor_tensor(st[t][:], window[t][:, whole], hop[t][:], ALU.subtract)

        out_codes = sb([P, S], U32, "out_codes")
        out_scales = sb([P, S], U8, "out_scales")
        out_rows = out_0.rearrange("(p t) j -> p t j", t=PACK)
        out_words = out_1[0].rearrange("p n r -> p (n r)").bitcast(I32)
        for c, (j0, w) in enumerate(OUT_CHUNKS):
            cols = slice(j0, j0 + w)
            result = sb([P, PACK, w], F32, "result%d" % c)
            result_side = sb([P, w, PACK], BF16, "result_side%d" % c)
            for t in range(PACK):
                far = ring.tile([P, w], F32, name="far", bufs=FAR_BUFS, align_bytes=64)
                nc.scalar.activation(far[:], st[t][:].indirect(entries(n3_t, j0, w)), ACT.Copy)
                nc.vector.tensor_tensor(result[:, t], st[t][:, cols], far[:], ALU.max)
            nc.sync.dma_start(out=out_rows[:, :, cols], in_=result[:])
            interleave(result_side[:], result[:])
            quantise(out_codes, out_scales, cols, result_side[:])
            queue = nc.scalar if j0 + w == S else nc.sync
            queue.dma_start(out=out_words[:, cols], in_=out_codes[:, cols].bitcast(I32))
        for q in range(QUADS):
            queue = nc.scalar if q % 2 else nc.sync
            queue.dma_start(
                out=out_2[0][4 * q : 4 * q + 4, :].bitcast(I32), in_=out_scales[32 * q : 32 * q + 4, :].bitcast(I32)
            )
